import numpy as np
import ml_dtypes


def mxq(x, axis, fmt="e4m3"):
    dtype, down = {"e4m3": (ml_dtypes.float8_e4m3fn, 7), "e5m2": (ml_dtypes.float8_e5m2, 14)}[fmt]
    v = np.moveaxis(np.asarray(x, np.float32).astype(ml_dtypes.bfloat16).astype(np.float64), axis, -1)
    blocks = v.reshape(v.shape[:-1] + (-1, 32))
    amax = np.abs(blocks).max(-1, keepdims=True)
    byte = np.maximum(np.where(amax > 0, np.frexp(amax)[1] - 1 + 127, 0) - down, 1)
    scale = np.exp2(byte - 127.0)
    codes = (blocks / scale).astype(np.float32).astype(dtype).astype(np.float64)
    return np.moveaxis((codes * scale).reshape(v.shape), -1, axis)


WIDE = False


def mx_kscale(k):
    if not WIDE:
        return np.ones(k)
    levels = np.array([10, -10, 5, -5, 0])
    if k % 512:
        return np.exp2(np.random.permutation(np.resize(levels, k // 32))).repeat(32)
    a = np.empty((k // 512, 16))
    for p in range(k // 512):
        a[p, :8] = np.random.permutation(np.resize(levels, 8))
        for g in range(8):
            far = levels[np.abs(levels - a[p, g]) >= 10]
            a[p, g + 8] = far[np.random.randint(len(far))]
    return np.exp2(a.ravel()).repeat(32)


def f64(x):
    return np.asarray(x).astype(np.float64)


def striped(idx):
    return np.tile(np.asarray(idx).reshape(-1, 16).T, (8, 1)).astype(np.uint16)


def unstriped(offs):
    return offs[:16].T.reshape(-1).astype(np.int64)


def striped8(idx):
    return np.asarray(idx).reshape(8, -1, 16).transpose(0, 2, 1).reshape(128, -1).astype(np.uint16)


def unstriped8(offs):
    return offs.reshape(8, 16, -1).transpose(0, 2, 1).reshape(8, -1).astype(np.int64)


def pick8(x, idx, run):
    r = np.arange(len(x))
    return x[r[:, None], idx[r % (8 * run) // run]]


E2M1 = np.array([0.0, 0.5, 1.0, 1.5, 2.0, 3.0, 4.0, 6.0, -0.0, -0.5, -1.0, -1.5, -2.0, -3.0, -4.0, -6.0])


def pack_weight(w, fmt):
    k, n = w.shape
    w = f64(np.asarray(w, np.float32).astype(ml_dtypes.bfloat16)).reshape(k // 32, 32, n)
    amax = np.abs(w).max(1)
    if fmt == "e4m3":
        byte = np.frexp(amax)[1] - 1 + 127 - 7
    else:
        mant, ex = np.frexp(amax / 6.0)
        byte = np.where(mant > 0.5, ex, ex - 1) + 127
    byte = np.clip(np.where(amax > 0, byte, 1), 1, 254)
    scaled = (w * np.exp2(127.0 - byte)[:, None, :]).reshape(k, n).astype(np.float32)
    by_word = np.ascontiguousarray(scaled.reshape(k // 512, 128, 4, n).transpose(0, 1, 3, 2))
    if fmt == "e4m3":
        words = by_word.astype(ml_dtypes.float8_e4m3fn).view(np.uint8)
    else:
        c = by_word.astype(ml_dtypes.float4_e2m1fn).view(np.uint8) & 0xF
        words = (c[..., 0::2] | (c[..., 1::2] << 4)).reshape(k // 512, 128, 2 * n)
    return np.ascontiguousarray(words), np.ascontiguousarray(byte.astype(np.uint8).reshape(k // 512, 16, n))


def unpack_weight(words, scales, fmt):
    g, _, n = scales.shape
    words = np.ascontiguousarray(words).reshape(g, 128, n, -1)
    if fmt == "e4m3":
        vals = words.view(ml_dtypes.float8_e4m3fn).astype(np.float64)
    else:
        nib = np.empty((g, 128, n, 4), np.uint8)
        nib[..., 0::2] = words & 0xF
        nib[..., 1::2] = words >> 4
        vals = E2M1[nib]
    vals = vals * np.repeat(np.exp2(scales.astype(np.float64) - 127.0), 8, axis=1)[..., None]
    return vals.transpose(0, 1, 3, 2).reshape(g * 512, n)


K, J, R, T, Z, M, O, N, U, E = 512, 512, 512, 1024, 512, 1024, 256, 256, 512, 128


def setup_inputs():
    n = np.random.standard_normal
    idx = np.random.permutation(T)[:J]
    idx2 = np.random.permutation(M)[:J]
    idx3 = np.stack([np.random.permutation(J)[:O] for _ in range(8)])
    idx4 = np.stack([np.random.permutation(U)[:O] for _ in range(8)])
    idx5 = np.stack([np.random.permutation(U)[:O] for _ in range(8)])
    idx6 = np.stack([np.random.permutation(U)[:E] for _ in range(8)])
    idx7 = np.stack([np.random.permutation(U)[:E] for _ in range(8)])
    fk = mx_kscale(K)
    fr = mx_kscale(R)
    fz = mx_kscale(Z)
    xtp = pack_weight(n((K, T)) * fk[:, None], "e4m3")
    wp = pack_weight(n((K, R)) * 1 / np.sqrt(K) / fk[:, None] * fr, "e2m1")
    xop = pack_weight(n((Z, M)) / fz[:, None], "e2m1")
    w2p = pack_weight(n((Z, R)) * 1 / np.sqrt(Z) * fz[:, None] * fr, "e4m3")
    wbp = pack_weight(n((R, N)) * 1 / np.sqrt(R) / fr[:, None], "e4m3")
    wop = pack_weight(n((R, N)) * 1 / np.sqrt(R) / fr[:, None], "e2m1")
    return {
        "xt_words": xtp[0],
        "xt_scales": xtp[1],
        "w_words": wp[0],
        "w_scales": wp[1],
        "xo_words": xop[0],
        "xo_scales": xop[1],
        "w2_words": w2p[0],
        "w2_scales": w2p[1],
        "sa": (np.random.uniform(0.5, 1.6, (R, 1))).astype(np.float32),
        "wb_words": wbp[0],
        "wb_scales": wbp[1],
        "wo_words": wop[0],
        "wo_scales": wop[1],
        "se": (np.random.uniform(0.5, 1.6, (N, 1))).astype(np.float32),
        "sf": (np.random.uniform(0.5, 1.6, (N, 1))).astype(np.float32),
        "offs": striped(idx),
        "offs2": striped(idx2),
        "offs3": striped8(idx3),
        "offs4": striped8(idx4),
        "offs5": striped8(idx5),
        "offs6": striped8(idx6),
        "offs7": striped8(idx7),
    }


def reference(xt_words, xt_scales, w_words, w_scales, xo_words, xo_scales, w2_words, w2_scales, sa, wb_words, wb_scales, wo_words, wo_scales, se, sf, offs, offs2, offs3, offs4, offs5, offs6, offs7):
    idx = unstriped(offs)
    idx2 = unstriped(offs2)
    idx3 = unstriped8(offs3)
    idx4 = unstriped8(offs4)
    idx5 = unstriped8(offs5)
    idx6 = unstriped8(offs6)
    idx7 = unstriped8(offs7)
    xtu = unpack_weight(xt_words, xt_scales, "e4m3")
    wu = unpack_weight(w_words, w_scales, "e2m1")
    xou = unpack_weight(xo_words, xo_scales, "e2m1")
    w2u = unpack_weight(w2_words, w2_scales, "e4m3")
    wbu = unpack_weight(wb_words, wb_scales, "e4m3")
    wou = unpack_weight(wo_words, wo_scales, "e2m1")
    xtidxg = xtu[:, idx]
    xoidx2g = xou[:, idx2]
    a = wu.T @ xtidxg + w2u.T @ xoidx2g
    g1 = np.maximum(a, 0.0)
    hid = pick8(g1, idx3, 64) * f64(sa)
    hidq = mxq(hid, 0, "e4m3")
    p = wbu.T @ hidq
    q = wou.T @ hidq
    m0 = np.zeros((N, U))
    m0[np.arange(N)[:, None], idx4[np.arange(N) % 128 // 16]] = p
    m1 = np.zeros((N, U))
    m1[np.arange(N)[:, None], idx5[np.arange(N) % 128 // 16]] = q
    m2 = np.maximum(m0, m1)
    y = pick8(m2, idx6, 16) * f64(se) - pick8(m1, idx7, 16) * f64(sf)
    return y

@@ -1,0 +1,208 @@
+from contextlib import ExitStack
+
+import concourse.mybir as mybir
+
+F32 = mybir.dt.float32
+BF16 = mybir.dt.bfloat16
+I32 = mybir.dt.int32
+U32 = mybir.dt.uint32
+U16 = mybir.dt.uint16
+U8 = mybir.dt.uint8
+FP8X4 = mybir.dt.float8_e4m3fn_x4
+FP4X4 = mybir.dt.float4_e2m1fn_x4
+ACT = mybir.ActivationFunctionType
+ALU = mybir.AluOpType
+
+P = 128
+PACK = 4
+J, R, T, M, O, N, U, E = 512, 512, 1024, 1024, 256, 256, 512, 128
+HALVES = 2
+JH = J // HALVES
+OH = O // HALVES
+NB = N // P
+
+FLOPS = 671088640
+
+
+def tile_picked_tokens_plain_bank_kept_outcomes_endreads_kernel(
+    tc, xt_words, xt_scales, w_words, w_scales, xo_words, xo_scales, w2_words, w2_scales, sa,
+    wb_words, wb_scales, wo_words, wo_scales, se, sf, offs, offs2, offs3, offs4, offs5, offs6, offs7, out,
+):
+    nc = tc.nc
+    with ExitStack() as ctx:
+        keep = ctx.enter_context(tc.tile_pool(name="keep", bufs=1))
+        psum = ctx.enter_context(tc.psum_pool(name="psum", bufs=1))
+
+        def sbuf(name, shape, dtype):
+            return keep.tile(shape, dtype, name=name, align_bytes=64)
+
+        def load_list(name, src):
+            tile = sbuf(name, [P, src.shape[1]], U16)
+            nc.sync.dma_start(tile[:], src)
+            return tile
+
+        def cleared_plane(name, width):
+            tile = sbuf(name, [P, width], U8)
+            nc.vector.memset(tile[:].bitcast(I32), 0)
+            return tile
+
+        def load_scale_rows(tile, src):
+            for q in range(4):
+                nc.sync.dma_start(tile[32 * q : 32 * q + 4, :].bitcast(I32), src[0, 4 * q : 4 * q + 4, :].bitcast(I32))
+
+        def load_fp8_words(name, src):
+            tile = sbuf(name, [P, src.shape[2]], I32)
+            nc.sync.dma_start(tile[:], src[0].rearrange("p n t -> p (n t)").bitcast(I32))
+            return tile
+
+        def load_fp4_words(name, src):
+            tile = sbuf(name, [P, src.shape[2] // 2], U16)
+            nc.sync.dma_start(tile[:].bitcast(I32), src[0].bitcast(I32))
+            return tile
+
+        def dealt(view):
+            return view.rearrange("p (t m) -> p m t", t=PACK)
+
+        def undealt(view):
+            return view.rearrange("p (m t) -> p m t", t=PACK)
+
+        xo_plane = cleared_plane("xo_plane", M)
+        w2_plane = cleared_plane("w2_plane", R)
+        xt_plane = cleared_plane("xt_plane", T)
+        w_plane = cleared_plane("w_plane", R)
+        wb_plane = cleared_plane("wb_plane", N)
+        wo_plane = cleared_plane("wo_plane", N)
+
+        list2 = load_list("list2", offs2)
+        load_scale_rows(xo_plane, xo_scales)
+        xo_codes = load_fp4_words("xo_codes", xo_words)
+        w2_codes = load_fp8_words("w2_codes", w2_words)
+        list1 = load_list("list1", offs)
+        load_scale_rows(w2_plane, w2_scales)
+        xt_codes = load_fp8_words("xt_codes", xt_words)
+        w_codes = load_fp4_words("w_codes", w_words)
+        load_scale_rows(xt_plane, xt_scales)
+        load_scale_rows(w_plane, w_scales)
+        list3 = load_list("list3", offs3)
+        sa_cols = sbuf("sa_cols", [P, PACK], F32)
+        nc.sync.dma_start(sa_cols[:], sa.rearrange("(p t) o -> p (t o)", t=PACK))
+        wo_codes = load_fp4_words("wo_codes", wo_words)
+        load_scale_rows(wo_plane, wo_scales)
+        wb_codes = load_fp8_words("wb_codes", wb_words)
+        load_scale_rows(wb_plane, wb_scales)
+        list5 = load_list("list5", offs5)
+        list4 = load_list("list4", offs4)
+        list7 = load_list("list7", offs7)
+        list6 = load_list("list6", offs6)
+        se_cols = sbuf("se_cols", [P, NB], F32)
+        sf_cols = sbuf("sf_cols", [P, NB], F32)
+        with nc.allow_non_contiguous_dma(reason="one value a partition for each block of 128 output features"):
+            nc.sync.dma_start(sf_cols[:], sf.rearrange("(b p) o -> p (b o)", p=P))
+            nc.sync.dma_start(se_cols[:], se.rearrange("(b p) o -> p (b o)", p=P))
+
+        page0 = [sbuf(f"page0_{b}", [P, U], F32) for b in range(NB)]
+        page1 = [sbuf(f"page1_{b}", [P, U], F32) for b in range(NB)]
+        for b in range(NB):
+            nc.vector.memset(page1[b][:], 0.0)
+            nc.vector.memset(page0[b][:], 0.0)
+
+        xo_plane_g = sbuf("xo_plane_g", [P, J], U8)
+        nc.vector.tensor_copy(xo_plane_g[:], xo_plane[:].indirect(list2[:]))
+        xo_codes_g = sbuf("xo_codes_g", [P, J], U16)
+        nc.vector.tensor_copy(xo_codes_g[:], xo_codes[:].indirect(list2[:]))
+
+        w2_codes_d = sbuf("w2_codes_d", [P, R], U32)
+        nc.scalar.copy(dealt(w2_codes_d[:]), undealt(w2_codes[:].bitcast(U32)))
+        w2_plane_d = sbuf("w2_plane_d", [P, R], U8)
+        nc.vector.tensor_copy(dealt(w2_plane_d[:]), undealt(w2_plane[:]))
+        w_codes_d = sbuf("w_codes_d", [P, R], U16)
+        nc.scalar.copy(dealt(w_codes_d[:]), undealt(w_codes[:]))
+
+        acc = {}
+        for h in range(HALVES):
+            slots = slice(h * JH, (h + 1) * JH)
+            for t in range(PACK):
+                cols = slice(t * P, (t + 1) * P)
+                acc[h, t] = psum.tile([P, JH], F32, name=f"acc{h}{t}", tag=f"bank{h}{t}")
+                nc.tensor.matmul_mx(
+                    out=acc[h, t][:],
+                    lhsT=w2_codes_d[:, cols].bitcast(FP8X4), lhsT_scale=w2_plane_d[:, cols],
+                    rhs=xo_codes_g[:, slots].bitcast(FP4X4), rhs_scale=xo_plane_g[:, slots],
+                    start=True, stop=False,
+                )
+
+        g1 = [sbuf(f"g1_{t}", [P, J], F32) for t in range(PACK)]
+        w_plane_d = sbuf("w_plane_d", [P, R], U8)
+        for h in range(HALVES):
+            slots = slice(h * JH, (h + 1) * JH)
+            entries = list1[:, h * JH // 16 : (h + 1) * JH // 16]
+            xt_codes_g = sbuf(f"xt_codes_g{h}", [P, JH], U32)
+            nc.vector.tensor_copy(xt_codes_g[:], xt_codes[:].bitcast(U32).indirect(entries))
+            xt_plane_g = sbuf(f"xt_plane_g{h}", [P, JH], U8)
+            nc.vector.tensor_copy(xt_plane_g[:], xt_plane[:].indirect(entries))
+            if h == 0:
+                nc.vector.tensor_copy(dealt(w_plane_d[:]), undealt(w_plane[:]))
+            for t in range(PACK):
+                cols = slice(t * P, (t + 1) * P)
+                nc.tensor.matmul_mx(
+                    out=acc[h, t][:],
+                    lhsT=w_codes_d[:, cols].bitcast(FP4X4), lhsT_scale=w_plane_d[:, cols],
+                    rhs=xt_codes_g[:].bitcast(FP8X4), rhs_scale=xt_plane_g[:],
+                    start=False, stop=True,
+                )
+        for h in range(HALVES):
+            slots = slice(h * JH, (h + 1) * JH)
+            for t in range(PACK):
+                if h == 0:
+                    nc.scalar.activation(g1[t][:, slots], acc[h, t][:], ACT.Relu)
+                else:
+                    nc.vector.tensor_scalar_max(g1[t][:, slots], acc[h, t][:], 0.0)
+
+        hid = [sbuf(f"hid{h}", [P, PACK, OH], BF16) for h in range(HALVES)]
+        for h in range(HALVES):
+            entries = list3[:, h * OH // 16 : (h + 1) * OH // 16]
+            for t in range(PACK):
+                nc.scalar.activation(hid[h][:, t, :], g1[t][:].indirect(entries), ACT.Copy, scale=sa_cols[:, t : t + 1])
+
+        outcome = {}
+        for h in range(HALVES):
+            grouped = sbuf(f"grouped{h}", [P, OH, PACK], BF16)
+            nc.vector.tensor_copy(
+                grouped[:].rearrange("p (c i) t -> p c t i", i=4),
+                hid[h][:].rearrange("p t (c i) -> p c t i", i=4),
+            )
+            hid_codes = sbuf(f"hid_codes{h}", [P, OH], U32)
+            hid_plane = sbuf(f"hid_plane{h}", [P, OH], U8)
+            nc.vector.quantize_mx(
+                out=hid_codes[:].bitcast(FP8X4), scales=hid_plane[:], in_=grouped[:].rearrange("p c t -> p (c t)")
+            )
+            for b in range(NB):
+                cols = slice(b * P, (b + 1) * P)
+                for second, (codes, plane) in (
+                    (1, (wo_codes[:, cols].bitcast(FP4X4), wo_plane[:, cols])),
+                    (0, (wb_codes[:, cols].bitcast(FP8X4), wb_plane[:, cols])),
+                ):
+                    bank = psum.tile([P, OH], F32, name=f"res{h}{b}{second}", tag=f"bank{h}{2 * b + second}")
+                    nc.tensor.matmul_mx(
+                        out=bank[:], lhsT=codes, lhsT_scale=plane,
+                        rhs=hid_codes[:].bitcast(FP8X4), rhs_scale=hid_plane[:], start=True, stop=True,
+                    )
+                    outcome[h, b, second] = sbuf(f"outcome{h}{b}{second}", [P, OH], F32)
+                    nc.vector.tensor_copy(outcome[h, b, second][:], bank[:])
+
+        for h in range(HALVES):
+            part = slice(h * OH // 16, (h + 1) * OH // 16)
+            for b in range(NB):
+                nc.scalar.activation(page1[b][:].indirect(list5[:, part]), outcome[h, b, 1][:], ACT.Copy)
+                nc.scalar.activation(page0[b][:].indirect(list4[:, part]), outcome[h, b, 0][:], ACT.Copy)
+
+        for b in range(NB):
+            larger = sbuf(f"larger{b}", [P, U], F32)
+            nc.vector.tensor_tensor(larger[:], page0[b][:], page1[b][:], ALU.max)
+            taken = sbuf(f"taken{b}", [P, E], F32)
+            nc.scalar.activation(taken[:], page1[b][:].indirect(list7[:]), ACT.Copy, scale=sf_cols[:, b : b + 1])
+            read = sbuf(f"read{b}", [P, E], F32)
+            nc.scalar.activation(read[:], larger[:].indirect(list6[:]), ACT.Copy, scale=se_cols[:, b : b + 1])
+            result = sbuf(f"result{b}", [P, E], F32)
+            nc.vector.tensor_tensor(result[:], read[:], taken[:], ALU.subtract)
+            nc.sync.dma_start(out[b * P : (b + 1) * P, :], result[:])

@@ -41,14 +41,15 @@ def tile_picked_tokens_plain_bank_kept_outcomes_endreads_kernel(
             nc.sync.dma_start(tile[:], src)
             return tile
 
-        def cleared_plane(name, width):
+        def load_plane(name, src, queue):
+            width = src.shape[2]
             tile = sbuf(name, [P, width], U8)
-            nc.vector.memset(tile[:].bitcast(I32), 0)
-            return tile
-
-        def load_scale_rows(tile, src):
             for q in range(4):
-                nc.sync.dma_start(tile[32 * q : 32 * q + 4, :].bitcast(I32), src[0, 4 * q : 4 * q + 4, :].bitcast(I32))
+                rows = src[0, 4 * q : 4 * q + 4, :].bitcast(I32)
+                queue.dma_start(
+                    tile[32 * q : 32 * q + 32, :].bitcast(I32), rows.unsqueeze(0).broadcast_to([8, 4, width // 4])
+                )
+            return tile
 
         def load_fp8_words(name, src):
             tile = sbuf(name, [P, src.shape[2]], I32)
@@ -66,39 +67,34 @@ def tile_picked_tokens_plain_bank_kept_outcomes_endreads_kernel(
         def undealt(view):
             return view.rearrange("p (m t) -> p m t", t=PACK)
 
-        xo_plane = cleared_plane("xo_plane", M)
-        w2_plane = cleared_plane("w2_plane", R)
-        xt_plane = cleared_plane("xt_plane", T)
-        w_plane = cleared_plane("w_plane", R)
-        wb_plane = cleared_plane("wb_plane", N)
-        wo_plane = cleared_plane("wo_plane", N)
-
         list2 = load_list("list2", offs2)
-        load_scale_rows(xo_plane, xo_scales)
+        xo_plane = load_plane("xo_plane", xo_scales, nc.sync)
         xo_codes = load_fp4_words("xo_codes", xo_words)
         w2_codes = load_fp8_words("w2_codes", w2_words)
         list1 = load_list("list1", offs)
-        load_scale_rows(w2_plane, w2_scales)
+        w2_plane = load_plane("w2_plane", w2_scales, nc.sync)
         xt_codes = load_fp8_words("xt_codes", xt_words)
         w_codes = load_fp4_words("w_codes", w_words)
-        load_scale_rows(xt_plane, xt_scales)
-        load_scale_rows(w_plane, w_scales)
+        w_plane = load_plane("w_plane", w_scales, nc.sync)
+        xt_plane = load_plane("xt_plane", xt_scales, nc.sync)
         list3 = load_list("list3", offs3)
-        sa_cols = sbuf("sa_cols", [P, PACK], F32)
-        nc.sync.dma_start(sa_cols[:], sa.rearrange("(p t) o -> p (t o)", t=PACK))
         wo_codes = load_fp4_words("wo_codes", wo_words)
-        load_scale_rows(wo_plane, wo_scales)
-        wb_codes = load_fp8_words("wb_codes", wb_words)
-        load_scale_rows(wb_plane, wb_scales)
+        wo_plane = load_plane("wo_plane", wo_scales, nc.sync)
         list5 = load_list("list5", offs5)
+        wb_codes = load_fp8_words("wb_codes", wb_words)
+        wb_plane = load_plane("wb_plane", wb_scales, nc.sync)
         list4 = load_list("list4", offs4)
         list7 = load_list("list7", offs7)
         list6 = load_list("list6", offs6)
+        sa_early = keep.tile([P, PACK], F32, name="sa_early", tag="held", align_bytes=64)
+        nc.gpsimd.dma_start(sa_early[:], sa.rearrange("(p t) o -> p (t o)", t=PACK))
+        sa_cols = sbuf("sa_cols", [P, PACK], F32)
+        nc.gpsimd.dma_start(sa_cols[:], sa.rearrange("(p t) o -> p (t o)", t=PACK))
         se_cols = sbuf("se_cols", [P, NB], F32)
         sf_cols = sbuf("sf_cols", [P, NB], F32)
         with nc.allow_non_contiguous_dma(reason="one value a partition for each block of 128 output features"):
-            nc.sync.dma_start(sf_cols[:], sf.rearrange("(b p) o -> p (b o)", p=P))
-            nc.sync.dma_start(se_cols[:], se.rearrange("(b p) o -> p (b o)", p=P))
+            nc.gpsimd.dma_start(sf_cols[:], sf.rearrange("(b p) o -> p (b o)", p=P))
+            nc.gpsimd.dma_start(se_cols[:], se.rearrange("(b p) o -> p (b o)", p=P))
 
         page0 = [sbuf(f"page0_{b}", [P, U], F32) for b in range(NB)]
         page1 = [sbuf(f"page1_{b}", [P, U], F32) for b in range(NB)]
@@ -132,37 +128,38 @@ def tile_picked_tokens_plain_bank_kept_outcomes_endreads_kernel(
                 )
 
         g1 = [sbuf(f"g1_{t}", [P, J], F32) for t in range(PACK)]
+        xt_codes_g = sbuf("xt_codes_g", [P, J], U32)
+        nc.vector.tensor_copy(xt_codes_g[:], xt_codes[:].bitcast(U32).indirect(list1[:]))
         w_plane_d = sbuf("w_plane_d", [P, R], U8)
+        nc.vector.tensor_copy(dealt(w_plane_d[:]), undealt(w_plane[:]))
         for h in range(HALVES):
             slots = slice(h * JH, (h + 1) * JH)
             entries = list1[:, h * JH // 16 : (h + 1) * JH // 16]
-            xt_codes_g = sbuf(f"xt_codes_g{h}", [P, JH], U32)
-            nc.vector.tensor_copy(xt_codes_g[:], xt_codes[:].bitcast(U32).indirect(entries))
             xt_plane_g = sbuf(f"xt_plane_g{h}", [P, JH], U8)
             nc.vector.tensor_copy(xt_plane_g[:], xt_plane[:].indirect(entries))
-            if h == 0:
-                nc.vector.tensor_copy(dealt(w_plane_d[:]), undealt(w_plane[:]))
             for t in range(PACK):
                 cols = slice(t * P, (t + 1) * P)
                 nc.tensor.matmul_mx(
                     out=acc[h, t][:],
                     lhsT=w_codes_d[:, cols].bitcast(FP4X4), lhsT_scale=w_plane_d[:, cols],
-                    rhs=xt_codes_g[:].bitcast(FP8X4), rhs_scale=xt_plane_g[:],
+                    rhs=xt_codes_g[:, slots].bitcast(FP8X4), rhs_scale=xt_plane_g[:],
                     start=False, stop=True,
                 )
         for h in range(HALVES):
             slots = slice(h * JH, (h + 1) * JH)
             for t in range(PACK):
-                if h == 0:
+                if h == 0 and t != 2:
                     nc.scalar.activation(g1[t][:, slots], acc[h, t][:], ACT.Relu)
                 else:
                     nc.vector.tensor_scalar_max(g1[t][:, slots], acc[h, t][:], 0.0)
 
-        hid = [sbuf(f"hid{h}", [P, PACK, OH], BF16) for h in range(HALVES)]
+        hid = []
         for h in range(HALVES):
             entries = list3[:, h * OH // 16 : (h + 1) * OH // 16]
+            hid.append(keep.tile([P, PACK, OH], BF16, name=f"hid{h}", tag="held" if h else "hid0", align_bytes=64))
             for t in range(PACK):
-                nc.scalar.activation(hid[h][:, t, :], g1[t][:].indirect(entries), ACT.Copy, scale=sa_cols[:, t : t + 1])
+                weight = sa_early if h == 0 and t < PACK - 1 else sa_cols
+                nc.scalar.activation(hid[h][:, t, :], g1[t][:].indirect(entries), ACT.Copy, scale=weight[:, t : t + 1])
 
         outcome = {}
         for h in range(HALVES):
@@ -176,15 +173,12 @@ def tile_picked_tokens_plain_bank_kept_outcomes_endreads_kernel(
             nc.vector.quantize_mx(
                 out=hid_codes[:].bitcast(FP8X4), scales=hid_plane[:], in_=grouped[:].rearrange("p c t -> p (c t)")
             )
-            for b in range(NB):
-                cols = slice(b * P, (b + 1) * P)
-                for second, (codes, plane) in (
-                    (1, (wo_codes[:, cols].bitcast(FP4X4), wo_plane[:, cols])),
-                    (0, (wb_codes[:, cols].bitcast(FP8X4), wb_plane[:, cols])),
-                ):
+            for second, codes, plane, fmt in ((1, wo_codes, wo_plane, FP4X4), (0, wb_codes, wb_plane, FP8X4)):
+                for b in range(NB):
+                    cols = slice(b * P, (b + 1) * P)
                     bank = psum.tile([P, OH], F32, name=f"res{h}{b}{second}", tag=f"bank{h}{2 * b + second}")
                     nc.tensor.matmul_mx(
-                        out=bank[:], lhsT=codes, lhsT_scale=plane,
+                        out=bank[:], lhsT=codes[:, cols].bitcast(fmt), lhsT_scale=plane[:, cols],
                         rhs=hid_codes[:].bitcast(FP8X4), rhs_scale=hid_plane[:], start=True, stop=True,
                     )
                     outcome[h, b, second] = sbuf(f"outcome{h}{b}{second}", [P, OH], F32)
@@ -194,6 +188,7 @@ def tile_picked_tokens_plain_bank_kept_outcomes_endreads_kernel(
             part = slice(h * OH // 16, (h + 1) * OH // 16)
             for b in range(NB):
                 nc.scalar.activation(page1[b][:].indirect(list5[:, part]), outcome[h, b, 1][:], ACT.Copy)
+            for b in range(NB):
                 nc.scalar.activation(page0[b][:].indirect(list4[:, part]), outcome[h, b, 0][:], ACT.Copy)
 
         for b in range(NB):

from contextlib import ExitStack

import concourse.mybir as mybir

F32 = mybir.dt.float32
BF16 = mybir.dt.bfloat16
I32 = mybir.dt.int32
U32 = mybir.dt.uint32
U16 = mybir.dt.uint16
U8 = mybir.dt.uint8
FP8X4 = mybir.dt.float8_e4m3fn_x4
FP4X4 = mybir.dt.float4_e2m1fn_x4
ACT = mybir.ActivationFunctionType
ALU = mybir.AluOpType

P = 128
PACK = 4
J, R, T, M, O, N, U, E = 512, 512, 1024, 1024, 256, 256, 512, 128
HALVES = 2
JH = J // HALVES
OH = O // HALVES
NB = N // P

FLOPS = 671088640


def tile_picked_tokens_plain_bank_kept_outcomes_endreads_kernel(
    tc, xt_words, xt_scales, w_words, w_scales, xo_words, xo_scales, w2_words, w2_scales, sa,
    wb_words, wb_scales, wo_words, wo_scales, se, sf, offs, offs2, offs3, offs4, offs5, offs6, offs7, out,
):
    nc = tc.nc
    with ExitStack() as ctx:
        keep = ctx.enter_context(tc.tile_pool(name="keep", bufs=1))
        psum = ctx.enter_context(tc.psum_pool(name="psum", bufs=1))

        def sbuf(name, shape, dtype):
            return keep.tile(shape, dtype, name=name, align_bytes=64)

        def load_list(name, src):
            tile = sbuf(name, [P, src.shape[1]], U16)
            nc.sync.dma_start(tile[:], src)
            return tile

        def load_plane(name, src, queue):
            width = src.shape[2]
            tile = sbuf(name, [P, width], U8)
            for q in range(4):
                rows = src[0, 4 * q : 4 * q + 4, :].bitcast(I32)
                queue.dma_start(
                    tile[32 * q : 32 * q + 32, :].bitcast(I32), rows.unsqueeze(0).broadcast_to([8, 4, width // 4])
                )
            return tile

        def load_fp8_words(name, src):
            tile = sbuf(name, [P, src.shape[2]], I32)
            nc.sync.dma_start(tile[:], src[0].rearrange("p n t -> p (n t)").bitcast(I32))
            return tile

        def load_fp4_words(name, src):
            tile = sbuf(name, [P, src.shape[2] // 2], U16)
            nc.sync.dma_start(tile[:].bitcast(I32), src[0].bitcast(I32))
            return tile

        def dealt(view):
            return view.rearrange("p (t m) -> p m t", t=PACK)

        def undealt(view):
            return view.rearrange("p (m t) -> p m t", t=PACK)

        list2 = load_list("list2", offs2)
        xo_plane = load_plane("xo_plane", xo_scales, nc.sync)
        xo_codes = load_fp4_words("xo_codes", xo_words)
        w2_codes = load_fp8_words("w2_codes", w2_words)
        list1 = load_list("list1", offs)
        w2_plane = load_plane("w2_plane", w2_scales, nc.sync)
        xt_codes = load_fp8_words("xt_codes", xt_words)
        w_codes = load_fp4_words("w_codes", w_words)
        w_plane = load_plane("w_plane", w_scales, nc.sync)
        xt_plane = load_plane("xt_plane", xt_scales, nc.sync)
        list3 = load_list("list3", offs3)
        wo_codes = load_fp4_words("wo_codes", wo_words)
        wo_plane = load_plane("wo_plane", wo_scales, nc.sync)
        list5 = load_list("list5", offs5)
        wb_codes = load_fp8_words("wb_codes", wb_words)
        wb_plane = load_plane("wb_plane", wb_scales, nc.sync)
        list4 = load_list("list4", offs4)
        list7 = load_list("list7", offs7)
        list6 = load_list("list6", offs6)
        sa_early = keep.tile([P, PACK], F32, name="sa_early", tag="held", align_bytes=64)
        nc.gpsimd.dma_start(sa_early[:], sa.rearrange("(p t) o -> p (t o)", t=PACK))
        sa_cols = sbuf("sa_cols", [P, PACK], F32)
        nc.gpsimd.dma_start(sa_cols[:], sa.rearrange("(p t) o -> p (t o)", t=PACK))
        se_cols = sbuf("se_cols", [P, NB], F32)
        sf_cols = sbuf("sf_cols", [P, NB], F32)
        with nc.allow_non_contiguous_dma(reason="one value a partition for each block of 128 output features"):
            nc.gpsimd.dma_start(sf_cols[:], sf.rearrange("(b p) o -> p (b o)", p=P))
            nc.gpsimd.dma_start(se_cols[:], se.rearrange("(b p) o -> p (b o)", p=P))

        page0 = [sbuf(f"page0_{b}", [P, U], F32) for b in range(NB)]
        page1 = [sbuf(f"page1_{b}", [P, U], F32) for b in range(NB)]
        for b in range(NB):
            nc.vector.memset(page1[b][:], 0.0)
            nc.vector.memset(page0[b][:], 0.0)

        xo_plane_g = sbuf("xo_plane_g", [P, J], U8)
        nc.vector.tensor_copy(xo_plane_g[:], xo_plane[:].indirect(list2[:]))
        xo_codes_g = sbuf("xo_codes_g", [P, J], U16)
        nc.vector.tensor_copy(xo_codes_g[:], xo_codes[:].indirect(list2[:]))

        w2_codes_d = sbuf("w2_codes_d", [P, R], U32)
        nc.scalar.copy(dealt(w2_codes_d[:]), undealt(w2_codes[:].bitcast(U32)))
        w2_plane_d = sbuf("w2_plane_d", [P, R], U8)
        nc.vector.tensor_copy(dealt(w2_plane_d[:]), undealt(w2_plane[:]))
        w_codes_d = sbuf("w_codes_d", [P, R], U16)
        nc.scalar.copy(dealt(w_codes_d[:]), undealt(w_codes[:]))

        acc = {}
        for h in range(HALVES):
            slots = slice(h * JH, (h + 1) * JH)
            for t in range(PACK):
                cols = slice(t * P, (t + 1) * P)
                acc[h, t] = psum.tile([P, JH], F32, name=f"acc{h}{t}", tag=f"bank{h}{t}")
                nc.tensor.matmul_mx(
                    out=acc[h, t][:],
                    lhsT=w2_codes_d[:, cols].bitcast(FP8X4), lhsT_scale=w2_plane_d[:, cols],
                    rhs=xo_codes_g[:, slots].bitcast(FP4X4), rhs_scale=xo_plane_g[:, slots],
                    start=True, stop=False,
                )

        g1 = [sbuf(f"g1_{t}", [P, J], F32) for t in range(PACK)]
        xt_codes_g = sbuf("xt_codes_g", [P, J], U32)
        nc.vector.tensor_copy(xt_codes_g[:], xt_codes[:].bitcast(U32).indirect(list1[:]))
        w_plane_d = sbuf("w_plane_d", [P, R], U8)
        nc.vector.tensor_copy(dealt(w_plane_d[:]), undealt(w_plane[:]))
        for h in range(HALVES):
            slots = slice(h * JH, (h + 1) * JH)
            entries = list1[:, h * JH // 16 : (h + 1) * JH // 16]
            xt_plane_g = sbuf(f"xt_plane_g{h}", [P, JH], U8)
            nc.vector.tensor_copy(xt_plane_g[:], xt_plane[:].indirect(entries))
            for t in range(PACK):
                cols = slice(t * P, (t + 1) * P)
                nc.tensor.matmul_mx(
                    out=acc[h, t][:],
                    lhsT=w_codes_d[:, cols].bitcast(FP4X4), lhsT_scale=w_plane_d[:, cols],
                    rhs=xt_codes_g[:, slots].bitcast(FP8X4), rhs_scale=xt_plane_g[:],
                    start=False, stop=True,
                )
        for h in range(HALVES):
            slots = slice(h * JH, (h + 1) * JH)
            for t in range(PACK):
                if h == 0 and t != 2:
                    nc.scalar.activation(g1[t][:, slots], acc[h, t][:], ACT.Relu)
                else:
                    nc.vector.tensor_scalar_max(g1[t][:, slots], acc[h, t][:], 0.0)

        hid = []
        for h in range(HALVES):
            entries = list3[:, h * OH // 16 : (h + 1) * OH // 16]
            hid.append(keep.tile([P, PACK, OH], BF16, name=f"hid{h}", tag="held" if h else "hid0", align_bytes=64))
            for t in range(PACK):
                weight = sa_early if h == 0 and t < PACK - 1 else sa_cols
                nc.scalar.activation(hid[h][:, t, :], g1[t][:].indirect(entries), ACT.Copy, scale=weight[:, t : t + 1])

        outcome = {}
        for h in range(HALVES):
            grouped = sbuf(f"grouped{h}", [P, OH, PACK], BF16)
            nc.vector.tensor_copy(
                grouped[:].rearrange("p (c i) t -> p c t i", i=4),
                hid[h][:].rearrange("p t (c i) -> p c t i", i=4),
            )
            hid_codes = sbuf(f"hid_codes{h}", [P, OH], U32)
            hid_plane = sbuf(f"hid_plane{h}", [P, OH], U8)
            nc.vector.quantize_mx(
                out=hid_codes[:].bitcast(FP8X4), scales=hid_plane[:], in_=grouped[:].rearrange("p c t -> p (c t)")
            )
            for second, codes, plane, fmt in ((1, wo_codes, wo_plane, FP4X4), (0, wb_codes, wb_plane, FP8X4)):
                for b in range(NB):
                    cols = slice(b * P, (b + 1) * P)
                    bank = psum.tile([P, OH], F32, name=f"res{h}{b}{second}", tag=f"bank{h}{2 * b + second}")
                    nc.tensor.matmul_mx(
                        out=bank[:], lhsT=codes[:, cols].bitcast(fmt), lhsT_scale=plane[:, cols],
                        rhs=hid_codes[:].bitcast(FP8X4), rhs_scale=hid_plane[:], start=True, stop=True,
                    )
                    outcome[h, b, second] = sbuf(f"outcome{h}{b}{second}", [P, OH], F32)
                    nc.vector.tensor_copy(outcome[h, b, second][:], bank[:])

        for h in range(HALVES):
            part = slice(h * OH // 16, (h + 1) * OH // 16)
            for b in range(NB):
                nc.scalar.activation(page1[b][:].indirect(list5[:, part]), outcome[h, b, 1][:], ACT.Copy)
            for b in range(NB):
                nc.scalar.activation(page0[b][:].indirect(list4[:, part]), outcome[h, b, 0][:], ACT.Copy)

        for b in range(NB):
            larger = sbuf(f"larger{b}", [P, U], F32)
            nc.vector.tensor_tensor(larger[:], page0[b][:], page1[b][:], ALU.max)
            taken = sbuf(f"taken{b}", [P, E], F32)
            nc.scalar.activation(taken[:], page1[b][:].indirect(list7[:]), ACT.Copy, scale=sf_cols[:, b : b + 1])
            read = sbuf(f"read{b}", [P, E], F32)
            nc.scalar.activation(read[:], larger[:].indirect(list6[:]), ACT.Copy, scale=se_cols[:, b : b + 1])
            result = sbuf(f"result{b}", [P, E], F32)
            nc.vector.tensor_tensor(result[:], read[:], taken[:], ALU.subtract)
            nc.sync.dma_start(out[b * P : (b + 1) * P, :], result[:])
